import numpy as np
import ml_dtypes


def mxq(x, axis, fmt="e4m3"):
    dtype, down = {"e4m3": (ml_dtypes.float8_e4m3fn, 7), "e5m2": (ml_dtypes.float8_e5m2, 14)}[fmt]
    v = np.moveaxis(np.asarray(x, np.float32).astype(ml_dtypes.bfloat16).astype(np.float64), axis, -1)
    blocks = v.reshape(v.shape[:-1] + (-1, 32))
    amax = np.abs(blocks).max(-1, keepdims=True)
    byte = np.maximum(np.where(amax > 0, np.frexp(amax)[1] - 1 + 127, 0) - down, 1)
    scale = np.exp2(byte - 127.0)
    codes = (blocks / scale).astype(np.float32).astype(dtype).astype(np.float64)
    return np.moveaxis((codes * scale).reshape(v.shape), -1, axis)


WIDE = False


def mx_kscale(k):
    if not WIDE:
        return np.ones(k)
    levels = np.array([10, -10, 5, -5, 0])
    if k % 512:
        return np.exp2(np.random.permutation(np.resize(levels, k // 32))).repeat(32)
    a = np.empty((k // 512, 16))
    for p in range(k // 512):
        a[p, :8] = np.random.permutation(np.resize(levels, 8))
        for g in range(8):
            far = levels[np.abs(levels - a[p, g]) >= 10]
            a[p, g + 8] = far[np.random.randint(len(far))]
    return np.exp2(a.ravel()).repeat(32)


def f64(x):
    return np.asarray(x).astype(np.float64)


def striped(idx):
    return np.tile(idx.reshape(-1, 16).T, (8, 1)).astype(np.uint16)


def unstriped(offs):
    return offs[:16].T.reshape(-1).astype(np.int64)


def striped8(idx):
    return np.concatenate([x.reshape(-1, 16).T for x in idx]).astype(np.uint16)


def runs(offs, k):
    lists = np.stack([offs[16 * r : 16 * r + 16].T.reshape(-1) for r in range(8)]).astype(np.int64)
    return lists[np.arange(k) % 512 // 64]


def pack_weight(w):
    k, n = w.shape
    w = f64(np.asarray(w, np.float32).astype(ml_dtypes.bfloat16)).reshape(k // 32, 32, n)
    amax = np.abs(w).max(1)
    byte = np.clip(np.where(amax > 0, np.frexp(amax)[1] - 1 + 127 - 7, 1), 1, 254)
    scaled = (w * np.exp2(127.0 - byte)[:, None, :]).reshape(k, n).astype(np.float32)
    words = np.ascontiguousarray(scaled.reshape(k // 512, 128, 4, n).transpose(0, 1, 3, 2)).astype(ml_dtypes.float8_e4m3fn).view(np.uint8)
    return words, np.ascontiguousarray(byte.astype(np.uint8).reshape(k // 512, 16, n))


def unpack_weight(words, scales):
    g, p, n, _ = words.shape
    vals = np.ascontiguousarray(words).view(ml_dtypes.float8_e4m3fn).astype(np.float64) * np.repeat(np.exp2(scales.astype(np.float64) - 127.0), 8, axis=1)[..., None]
    return vals.transpose(0, 1, 3, 2).reshape(g * 512, n)


E2M1 = np.array([0.0, 0.5, 1.0, 1.5, 2.0, 3.0, 4.0, 6.0, -0.0, -0.5, -1.0, -1.5, -2.0, -3.0, -4.0, -6.0])


def pack_fp4(w):
    k, n = w.shape
    w = f64(np.asarray(w, np.float32).astype(ml_dtypes.bfloat16)).reshape(k // 32, 32, n)
    amax = np.abs(w).max(1)
    mant, ex = np.frexp(amax / 6.0)
    byte = np.clip(np.where(amax > 0, np.where(mant > 0.5, ex, ex - 1) + 127, 1), 1, 254)
    scaled = (w * np.exp2(127.0 - byte)[:, None, :]).reshape(k, n).astype(np.float32)
    c = np.ascontiguousarray(scaled.reshape(k // 512, 128, 4, n).transpose(0, 1, 3, 2)).astype(ml_dtypes.float4_e2m1fn).view(np.uint8) & 0xF
    words = (c[..., 0::2] | (c[..., 1::2] << 4)).reshape(k // 512, 128, 2 * n)
    return np.ascontiguousarray(words), np.ascontiguousarray(byte.astype(np.uint8).reshape(k // 512, 16, n))


def unpack_fp4(words, scales):
    g, _, n = scales.shape
    words = np.ascontiguousarray(words).reshape(g, 128, n, 2)
    nib = np.empty((g, 128, n, 4), np.uint8)
    nib[..., 0::2] = words & 0xF
    nib[..., 1::2] = words >> 4
    vals = E2M1[nib] * np.repeat(np.exp2(scales.astype(np.float64) - 127.0), 8, axis=1)[..., None]
    return vals.transpose(0, 1, 3, 2).reshape(g * 512, n)


def sigmoid(v):
    return 1.0 / (1.0 + np.exp(-np.maximum(v, -700.0)))


K, T, S, H, W, G = 512, 1024, 256, 512, 128, 2048


def setup_inputs():
    n = np.random.standard_normal
    s = mx_kscale(K)[:, None]
    packed_xT = pack_weight(n((K, T)) * s)
    packed_w1 = pack_fp4(n((K, H)) / np.sqrt(K) / s)
    packed_dT = pack_weight(n((K, G)) / s)
    perm = np.random.permutation(S)
    return {
        "x_words": packed_xT[0],
        "x_scales": packed_xT[1],
        "w1_words": packed_w1[0],
        "w1_scales": packed_w1[1],
        "gs": (np.random.uniform(0.5, 1.5, (K, 1)) * s).astype(np.float32),
        "d_words": packed_dT[0],
        "d_scales": packed_dT[1],
        "sl": np.random.uniform(1.0, 2.0, (H, 1)).astype(np.float32),
        "th": (0.5 * n((H, 1))).astype(np.float32),
        "offs": striped(np.random.permutation(T)[:S]),
        "n1": striped(perm[:W]),
        "n2": striped(perm[W:]),
        "n3": striped(np.random.permutation(S)),
        "k1": striped8(np.random.randint(0, G, (8, H))),
        "k2": striped8(np.random.randint(0, G, (8, H))),
        "hz": striped8(np.random.randint(0, T, (8, S))),
        "n4": striped8(np.stack([np.random.permutation(S) for _ in range(8)])),
        "n5": striped8(np.stack([np.random.permutation(S) for _ in range(8)])),
    }


def reference(x_words, x_scales, w1_words, w1_scales, gs, d_words, d_scales, sl, th, offs, n1, n2, n3, k1, k2, hz, n4, n5):
    d_k1 = unpack_weight(d_words, d_scales)[np.arange(K)[:, None], runs(k1, K)]
    xq = unpack_weight(x_words, x_scales)[:, unstriped(offs)]
    y = unpack_fp4(w1_words, w1_scales).T @ xq
    pa = y[:, unstriped(n1)]
    pb = y[:, unstriped(n2)]
    rb = pa - pb
    ra = pa + pb
    ds = np.zeros((H, S))
    ds[:, unstriped(n1)] = ra
    dt = ds.copy()
    dt[:, unstriped(n2)] = rb
    z = f64(gs) * (np.maximum(dt, dt[:, unstriped(n3)]))
    d_k2 = unpack_weight(d_words, d_scales)[np.arange(K)[:, None], runs(k2, K)]
    x_hz = unpack_weight(x_words, x_scales)[np.arange(K)[:, None], runs(hz, K)]
    h = 0.0625 * ((d_k1.T @ mxq(z, 0, "e4m3") + d_k2.T @ x_hz))
    st = np.maximum(h, h[np.arange(H)[:, None], runs(n4, H)])
    sg = sigmoid(f64(sl) * (st[np.arange(H)[:, None], runs(n5, H)] - f64(th)))
    return st * sg

@@ -1,0 +1,268 @@
+from contextlib import ExitStack
+
+import concourse.mybir as mybir
+
+K, T, S, H, W, G = 512, 1024, 256, 512, 128, 2048
+FLOPS = 2 * K * H * S * 3
+
+F32 = mybir.dt.float32
+BF16 = mybir.dt.bfloat16
+I32 = mybir.dt.int32
+U32 = mybir.dt.uint32
+U16 = mybir.dt.uint16
+U8 = mybir.dt.uint8
+FP8X4 = mybir.dt.float8_e4m3fn_x4
+FP4X4 = mybir.dt.float4_e2m1fn_x4
+ALU = mybir.AluOpType
+ACT = mybir.ActivationFunctionType
+
+P = 128
+PACK = 4
+QUADRANT = 32
+GROUP = 16
+DT_COLS = S + 16
+PIECE = 512
+HALF = S // 2
+
+
+def tile_picked_cmixhhaarhehh_none_p_kernel(
+    tc, x_words, x_scales, w1_words, w1_scales, gs, d_words, d_scales, sl, th, offs, n1, n2, n3, k1, k2, hz, n4, n5, out
+):
+    nc = tc.nc
+    with ExitStack() as ctx:
+        keep = ctx.enter_context(tc.tile_pool(name="keep", bufs=1))
+        psum = ctx.enter_context(tc.psum_pool(name="psum", bufs=1))
+
+        def sbuf(name, cols, dtype):
+            return keep.tile([P, cols], dtype, name=name, align_bytes=64)
+
+        def load_list(name, source):
+            tile = keep.tile(list(source.shape), U16, name=name)
+            nc.sync.dma_start(tile[:], source)
+            return tile
+
+        def zeroed_bytes(name, cols):
+            tile = sbuf(name, cols, U8)
+            nc.vector.memset(tile[:].bitcast(I32), 0)
+            return tile
+
+        def load_scale_rows(tile, scales, q):
+            rows = scales[0, PACK * q : PACK * (q + 1), :].bitcast(I32)
+            nc.sync.dma_start(
+                tile[QUADRANT * q : QUADRANT * (q + 1), :].bitcast(I32),
+                rows.unsqueeze(0).to_broadcast([QUADRANT // PACK, PACK, rows.shape[1]]),
+            )
+
+        def load_run_rows(tile, scales):
+            rows = scales[0].bitcast(I32)
+            nc.sync.dma_start(tile[:].bitcast(I32), rows.unsqueeze(1).to_broadcast([16, 8, rows.shape[1]]))
+
+        def place_run_rows(plane, gathered):
+            for u in range(2):
+                for e in range(2):
+                    nc.sync.dma_start(
+                        plane[2 * u + e : P : QUADRANT, :].bitcast(I32),
+                        gathered[GROUP * u + 8 * e : P : QUADRANT, :].bitcast(I32),
+                    )
+
+        def gather_pieces(dst, window, offsets, count):
+            for c in range(0, count, PIECE):
+                nc.vector.tensor_copy(dst[:, c : c + PIECE], window[:].indirect(offsets[:, c // 16 : (c + PIECE) // 16]))
+
+        xs_one = sbuf("xs_one", T, U8)
+        w1s = sbuf("w1s", H, U8)
+        xw = sbuf("xw", T, U32)
+        w1w = sbuf("w1w", H, U16)
+        offs_t = load_list("offs_t", offs)
+        for r in range(2):
+            load_scale_rows(xs_one, x_scales, r)
+        nc.sync.dma_start(xw[:].bitcast(I32), x_words[0].rearrange("p n t -> p (n t)").bitcast(I32))
+        for r in range(2, PACK):
+            load_scale_rows(xs_one, x_scales, r)
+        nc.sync.dma_start(w1w[:].bitcast(I32), w1_words[0].bitcast(I32))
+        for r in range(PACK):
+            load_scale_rows(w1s, w1_scales, r)
+        hz_t = load_list("hz_t", hz)
+        xs_runs = sbuf("xs_runs", T, U8)
+        load_run_rows(xs_runs, x_scales)
+        n1_t = load_list("n1_t", n1)
+        n2_t = load_list("n2_t", n2)
+        ds_runs = sbuf("ds_runs", G, U8)
+        load_run_rows(ds_runs, d_scales)
+        k1_t = load_list("k1_t", k1)
+        k2_t = load_list("k2_t", k2)
+        dw = sbuf("dw", G, U32)
+        nc.sync.dma_start(dw[:].bitcast(I32), d_words[0].rearrange("p n t -> p (n t)").bitcast(I32))
+        n3_t = load_list("n3_t", n3)
+        n4_t = load_list("n4_t", n4)
+        n5_t = load_list("n5_t", n5)
+        gs_t = sbuf("gs_t", PACK, F32)
+        sl_t = sbuf("sl_t", PACK, F32)
+        th_t = sbuf("th_t", PACK, F32)
+        for tile, source in ((gs_t, gs), (sl_t, sl), (th_t, th)):
+            nc.gpsimd.dma_start(tile[:], source.rearrange("(p t) o -> p (t o)", t=PACK))
+
+        dt = [sbuf("dt%d" % t, DT_COLS, F32) for t in range(PACK)]
+        for t in range(PACK):
+            nc.vector.memset(dt[t][:], 0.0)
+        d_plane = zeroed_bytes("d_plane", 2 * H)
+        hz_plane = zeroed_bytes("hz_plane", S)
+
+        w1w_dealt = sbuf("w1w_dealt", H, U16)
+        nc.scalar.copy(
+            w1w_dealt[:].rearrange("p (t c i) -> p c t i", t=PACK, i=8),
+            w1w[:].rearrange("p (c i t) -> p c t i", t=PACK, i=8),
+        )
+        w1s_dealt = sbuf("w1s_dealt", H, U8)
+        w1s_by_tile = w1s[:].rearrange("p (m t) -> p t m", t=PACK)
+        nc.vector.tensor_copy(w1s_dealt[:, :P], w1s_by_tile[:, 0, :])
+        nc.vector.tensor_copy(w1s_dealt[:, P:].rearrange("p (t m) -> p t m", m=P), w1s_by_tile[:, 1:, :])
+        xq_scales = sbuf("xq_scales", S, U8)
+        xq_words = sbuf("xq_words", S, U32)
+        nc.vector.tensor_copy(xq_scales[:], xs_one[:].indirect(offs_t[:]))
+        nc.vector.tensor_copy(xq_words[:], xw[:].indirect(offs_t[:]))
+
+        y = [sbuf("y%d" % t, S, F32) for t in range(PACK)]
+        h_win = [sbuf("h_win%d" % t, 2 * S, F32) for t in range(PACK)]
+        st_win = [sbuf("st_win%d" % t, 2 * S, F32) for t in range(PACK)]
+        sums = [sbuf("sums%d" % t, S, F32) for t in range(PACK)]
+        partner = [sbuf("partner%d" % t, S, F32) for t in range(PACK)]
+        larger = [sbuf("larger%d" % t, S, F32) for t in range(PACK)]
+        z_planes = keep.tile([P, PACK, S], BF16, name="z_planes", align_bytes=64)
+
+        def project(t):
+            bank = psum.tile([P, S], F32, name="y_bank%d" % t)
+            nc.tensor.matmul_mx(
+                out=bank[:],
+                lhsT=w1w_dealt[:, t * P : (t + 1) * P].bitcast(FP4X4),
+                lhsT_scale=w1s_dealt[:, t * P : (t + 1) * P],
+                rhs=xq_words[:].bitcast(FP8X4),
+                rhs_scale=xq_scales[:],
+                start=True,
+                stop=True,
+            )
+            if t == 0:
+                nc.scalar.copy(y[t][:], bank[:])
+            else:
+                nc.vector.tensor_copy(y[t][:], bank[:])
+
+        def pair_up(t):
+            pa = h_win[t][:, S : S + W]
+            pb = h_win[t][:, S + W : 2 * S]
+            nc.scalar.activation(pa, y[t][:].indirect(n1_t[:]), ACT.Copy)
+            nc.scalar.activation(pb, y[t][:].indirect(n2_t[:]), ACT.Copy)
+            nc.vector.tensor_tensor(sums[t][:, :W], pa, pb, ALU.add)
+            nc.vector.tensor_tensor(sums[t][:, W:], pa, pb, ALU.subtract)
+
+        def put_back(t):
+            nc.scalar.activation(dt[t][:].indirect(n1_t[:]), sums[t][:, :W], ACT.Copy)
+            nc.scalar.activation(dt[t][:].indirect(n2_t[:]), sums[t][:, W:], ACT.Copy)
+
+        def weigh(t, lo, hi):
+            nc.scalar.activation(partner[t][:, lo:hi], dt[t][:].indirect(n3_t[:, lo // 16 : hi // 16]), ACT.Copy)
+            nc.vector.tensor_tensor(larger[t][:, lo:hi], dt[t][:, lo:hi], partner[t][:, lo:hi], ALU.max)
+            nc.vector.tensor_scalar(z_planes[:, t, lo:hi], larger[t][:, lo:hi], gs_t[:, t : t + 1], None, ALU.mult)
+
+        for t in range(PACK):
+            project(t)
+        last = PACK - 1
+        for t in range(PACK):
+            pair_up(t)
+        for t in range(PACK):
+            put_back(t)
+            if t > 0:
+                weigh(t - 1, 0, S)
+
+        hz_bytes = sbuf("hz_bytes", S, U8)
+        nc.vector.tensor_copy(hz_bytes[:], xs_runs[:].indirect(hz_t[:]))
+        place_run_rows(hz_plane, hz_bytes)
+        hz_words = sbuf("hz_words", S, U32)
+        nc.vector.tensor_copy(hz_words[:], xw[:].indirect(hz_t[:]))
+        d_bytes = sbuf("d_bytes", 2 * H, U8)
+        gather_pieces(d_bytes[:, :H], ds_runs, k1_t, H)
+        gather_pieces(d_bytes[:, H:], ds_runs, k2_t, H)
+        d_bytes_dealt = sbuf("d_bytes_dealt", 2 * H, U8)
+        for a in range(2):
+            nc.vector.tensor_copy(
+                d_bytes_dealt[:, a * H : (a + 1) * H].rearrange("p (t c i) -> p c t i", t=PACK, i=16),
+                d_bytes[:, a * H : (a + 1) * H].rearrange("p (c i t) -> p c t i", t=PACK, i=16),
+            )
+        place_run_rows(d_plane, d_bytes_dealt)
+        d_dealt = []
+        for name, codes in (("d2", k2_t), ("d1", k1_t)):
+            picked = sbuf(name + "_picked", H, U32)
+            gather_pieces(picked, dw, codes, H)
+            dealt = sbuf(name + "_dealt", H, U32)
+            nc.vector.tensor_copy(
+                dealt[:].bitcast(I32).rearrange("p (t c i) -> p c t i", t=PACK, i=4),
+                picked[:].bitcast(I32).rearrange("p (c i t) -> p c t i", t=PACK, i=4),
+            )
+            d_dealt.append(dealt)
+        d2_dealt, d1_dealt = d_dealt
+        slope_times_threshold = sbuf("slope_times_threshold", PACK, F32)
+        bias = sbuf("bias", PACK, F32)
+        nc.gpsimd.tensor_tensor(slope_times_threshold[:], sl_t[:], th_t[:], ALU.mult)
+        nc.gpsimd.tensor_scalar(bias[:], slope_times_threshold[:], -1.0, 0.0, ALU.mult, ALU.add)
+
+        h_banks = [psum.tile([P, S], F32, name="h_bank%d" % t) for t in range(PACK)]
+        for t in range(PACK):
+            nc.tensor.matmul_mx(
+                out=h_banks[t][:],
+                lhsT=d2_dealt[:, t * P : (t + 1) * P].bitcast(FP8X4),
+                lhsT_scale=d_plane[:, H + t * P : H + (t + 1) * P],
+                rhs=hz_words[:].bitcast(FP8X4),
+                rhs_scale=hz_plane[:],
+                start=True,
+                stop=False,
+            )
+
+        for half in range(2):
+            lo, hi = half * HALF, (half + 1) * HALF
+            weigh(last, lo, hi)
+            z_grouped = sbuf("z_grouped%d" % half, HALF * PACK, BF16)
+            nc.vector.tensor_copy(
+                z_grouped[:].rearrange("p (c i t) -> p c t i", t=PACK, i=4),
+                z_planes[:, :, lo:hi].rearrange("p t (c i) -> p c t i", i=4),
+            )
+            z_words = sbuf("z_words%d" % half, HALF, U32)
+            z_scales = sbuf("z_scales%d" % half, HALF, U8)
+            nc.vector.quantize_mx(out=z_words[:].bitcast(FP8X4), scales=z_scales[:], in_=z_grouped[:])
+            for t in range(PACK):
+                nc.tensor.matmul_mx(
+                    out=h_banks[t][:, lo:hi],
+                    lhsT=d1_dealt[:, t * P : (t + 1) * P].bitcast(FP8X4),
+                    lhsT_scale=d_plane[:, t * P : (t + 1) * P],
+                    rhs=z_words[:].bitcast(FP8X4),
+                    rhs_scale=z_scales[:],
+                    start=False,
+                    stop=(half == 1),
+                )
+
+        out_rows = out.rearrange("(p t) s -> p t s", t=PACK)
+        gates = [sbuf("gates%d" % t, S, F32) for t in range(PACK)]
+        result = [sbuf("result%d" % t, S, F32) for t in range(PACK)]
+
+        def take_larger(t):
+            if t == 0:
+                nc.scalar.activation(h_win[t][:, :S], h_banks[t][:], ACT.Copy, scale=0.0625)
+            else:
+                nc.vector.tensor_scalar(h_win[t][:, :S], h_banks[t][:], 0.0625, None, ALU.mult)
+            nc.scalar.activation(st_win[t][:, S:], h_win[t][:].indirect(n4_t[:]), ACT.Copy)
+            nc.vector.tensor_tensor(st_win[t][:, :S], h_win[t][:, :S], st_win[t][:, S:], ALU.max)
+
+        def gate_and_store(t):
+            nc.scalar.activation(
+                gates[t][:],
+                st_win[t][:].indirect(n5_t[:]),
+                ACT.Sigmoid,
+                bias=bias[:, t : t + 1],
+                scale=sl_t[:, t : t + 1],
+            )
+            nc.vector.tensor_tensor(result[t][:], st_win[t][:, :S], gates[t][:], ALU.mult)
+            nc.sync.dma_start(out_rows[:, t, :], result[t][:])
+
+        take_larger(0)
+        for t in range(PACK):
+            if t < last:
+                take_larger(t + 1)
+            gate_and_store(t)

@@ -108,6 +108,11 @@ def tile_picked_cmixhhaarhehh_none_p_kernel(
         d_plane = zeroed_bytes("d_plane", 2 * H)
         hz_plane = zeroed_bytes("hz_plane", S)
 
+        warm_in = sbuf("warm_in", 1, F32)
+        warm_out = sbuf("warm_out", 1, F32)
+        nc.vector.memset(warm_in[:], 0.0)
+        nc.scalar.activation(warm_out[:], warm_in[:], ACT.Sigmoid)
+
         w1w_dealt = sbuf("w1w_dealt", H, U16)
         nc.scalar.copy(
             w1w_dealt[:].rearrange("p (t c i) -> p c t i", t=PACK, i=8),

@@ -21,7 +21,6 @@ PACK = 4
 QUADRANT = 32
 GROUP = 16
 DT_COLS = S + 16
-PIECE = 512
 HALF = S // 2
 
 
@@ -33,8 +32,8 @@ def tile_picked_cmixhhaarhehh_none_p_kernel(
         keep = ctx.enter_context(tc.tile_pool(name="keep", bufs=1))
         psum = ctx.enter_context(tc.psum_pool(name="psum", bufs=1))
 
-        def sbuf(name, cols, dtype):
-            return keep.tile([P, cols], dtype, name=name, align_bytes=64)
+        def sbuf(name, cols, dtype, tag=None):
+            return keep.tile([P, cols], dtype, name=name, tag=tag or name, align_bytes=64)
 
         def load_list(name, source):
             tile = keep.tile(list(source.shape), U16, name=name)
@@ -65,42 +64,33 @@ def tile_picked_cmixhhaarhehh_none_p_kernel(
                         gathered[GROUP * u + 8 * e : P : QUADRANT, :].bitcast(I32),
                     )
 
-        def gather_pieces(dst, window, offsets, count):
-            for c in range(0, count, PIECE):
-                nc.vector.tensor_copy(dst[:, c : c + PIECE], window[:].indirect(offsets[:, c // 16 : (c + PIECE) // 16]))
-
         xs_one = sbuf("xs_one", T, U8)
         w1s = sbuf("w1s", H, U8)
         xw = sbuf("xw", T, U32)
         w1w = sbuf("w1w", H, U16)
         offs_t = load_list("offs_t", offs)
-        for r in range(2):
+        for r in range(PACK):
             load_scale_rows(xs_one, x_scales, r)
         nc.sync.dma_start(xw[:].bitcast(I32), x_words[0].rearrange("p n t -> p (n t)").bitcast(I32))
-        for r in range(2, PACK):
-            load_scale_rows(xs_one, x_scales, r)
         nc.sync.dma_start(w1w[:].bitcast(I32), w1_words[0].bitcast(I32))
         for r in range(PACK):
             load_scale_rows(w1s, w1_scales, r)
+        n1_t = load_list("n1_t", n1)
+        n2_t = load_list("n2_t", n2)
+        n3_t = load_list("n3_t", n3)
         hz_t = load_list("hz_t", hz)
         xs_runs = sbuf("xs_runs", T, U8)
         load_run_rows(xs_runs, x_scales)
-        n1_t = load_list("n1_t", n1)
-        n2_t = load_list("n2_t", n2)
         ds_runs = sbuf("ds_runs", G, U8)
         load_run_rows(ds_runs, d_scales)
         k1_t = load_list("k1_t", k1)
         k2_t = load_list("k2_t", k2)
         dw = sbuf("dw", G, U32)
         nc.sync.dma_start(dw[:].bitcast(I32), d_words[0].rearrange("p n t -> p (n t)").bitcast(I32))
-        n3_t = load_list("n3_t", n3)
         n4_t = load_list("n4_t", n4)
         n5_t = load_list("n5_t", n5)
         gs_t = sbuf("gs_t", PACK, F32)
-        sl_t = sbuf("sl_t", PACK, F32)
-        th_t = sbuf("th_t", PACK, F32)
-        for tile, source in ((gs_t, gs), (sl_t, sl), (th_t, th)):
-            nc.gpsimd.dma_start(tile[:], source.rearrange("(p t) o -> p (t o)", t=PACK))
+        nc.gpsimd.dma_start(gs_t[:], gs.rearrange("(p t) o -> p (t o)", t=PACK))
 
         dt = [sbuf("dt%d" % t, DT_COLS, F32) for t in range(PACK)]
         for t in range(PACK):
@@ -114,10 +104,9 @@ def tile_picked_cmixhhaarhehh_none_p_kernel(
         nc.scalar.activation(warm_out[:], warm_in[:], ACT.Sigmoid)
 
         w1w_dealt = sbuf("w1w_dealt", H, U16)
-        nc.scalar.copy(
-            w1w_dealt[:].rearrange("p (t c i) -> p c t i", t=PACK, i=8),
-            w1w[:].rearrange("p (c i t) -> p c t i", t=PACK, i=8),
-        )
+        w1w_by_tile = w1w[:].rearrange("p (m t) -> p t m", t=PACK)
+        nc.scalar.copy(w1w_dealt[:, :P], w1w_by_tile[:, 0, :])
+        nc.scalar.copy(w1w_dealt[:, P:].rearrange("p (t m) -> p t m", m=P), w1w_by_tile[:, 1:, :])
         w1s_dealt = sbuf("w1s_dealt", H, U8)
         w1s_by_tile = w1s[:].rearrange("p (m t) -> p t m", t=PACK)
         nc.vector.tensor_copy(w1s_dealt[:, :P], w1s_by_tile[:, 0, :])
@@ -130,10 +119,9 @@ def tile_picked_cmixhhaarhehh_none_p_kernel(
         y = [sbuf("y%d" % t, S, F32) for t in range(PACK)]
         h_win = [sbuf("h_win%d" % t, 2 * S, F32) for t in range(PACK)]
         st_win = [sbuf("st_win%d" % t, 2 * S, F32) for t in range(PACK)]
-        sums = [sbuf("sums%d" % t, S, F32) for t in range(PACK)]
-        partner = [sbuf("partner%d" % t, S, F32) for t in range(PACK)]
-        larger = [sbuf("larger%d" % t, S, F32) for t in range(PACK)]
-        z_planes = keep.tile([P, PACK, S], BF16, name="z_planes", align_bytes=64)
+        pairs = [sbuf("pairs%d" % u, 2 * S, F32) for u in range(2)]
+        z_grouped = sbuf("z_grouped", S * PACK, BF16)
+        z_planes = z_grouped[:].rearrange("p (s t) -> p t s", t=PACK)
 
         def project(t):
             bank = psum.tile([P, S], F32, name="y_bank%d" % t)
@@ -151,63 +139,96 @@ def tile_picked_cmixhhaarhehh_none_p_kernel(
             else:
                 nc.vector.tensor_copy(y[t][:], bank[:])
 
-        def pair_up(t):
-            pa = h_win[t][:, S : S + W]
-            pb = h_win[t][:, S + W : 2 * S]
-            nc.scalar.activation(pa, y[t][:].indirect(n1_t[:]), ACT.Copy)
-            nc.scalar.activation(pb, y[t][:].indirect(n2_t[:]), ACT.Copy)
-            nc.vector.tensor_tensor(sums[t][:, :W], pa, pb, ALU.add)
-            nc.vector.tensor_tensor(sums[t][:, W:], pa, pb, ALU.subtract)
-
-        def put_back(t):
-            nc.scalar.activation(dt[t][:].indirect(n1_t[:]), sums[t][:, :W], ACT.Copy)
-            nc.scalar.activation(dt[t][:].indirect(n2_t[:]), sums[t][:, W:], ACT.Copy)
-
-        def weigh(t, lo, hi):
-            nc.scalar.activation(partner[t][:, lo:hi], dt[t][:].indirect(n3_t[:, lo // 16 : hi // 16]), ACT.Copy)
-            nc.vector.tensor_tensor(larger[t][:, lo:hi], dt[t][:, lo:hi], partner[t][:, lo:hi], ALU.max)
-            nc.vector.tensor_scalar(z_planes[:, t, lo:hi], larger[t][:, lo:hi], gs_t[:, t : t + 1], None, ALU.mult)
-
         for t in range(PACK):
             project(t)
         last = PACK - 1
         for t in range(PACK):
-            pair_up(t)
-        for t in range(PACK):
-            put_back(t)
-            if t > 0:
-                weigh(t - 1, 0, S)
+            u, start = t // 2, t % 2 * S
+            nc.scalar.activation(pairs[u][:, start : start + W], y[t][:].indirect(n1_t[:]), ACT.Copy)
+            nc.scalar.activation(pairs[u][:, start + W : start + S], y[t][:].indirect(n2_t[:]), ACT.Copy)
 
         hz_bytes = sbuf("hz_bytes", S, U8)
         nc.vector.tensor_copy(hz_bytes[:], xs_runs[:].indirect(hz_t[:]))
-        place_run_rows(hz_plane, hz_bytes)
         hz_words = sbuf("hz_words", S, U32)
         nc.vector.tensor_copy(hz_words[:], xw[:].indirect(hz_t[:]))
-        d_bytes = sbuf("d_bytes", 2 * H, U8)
-        gather_pieces(d_bytes[:, :H], ds_runs, k1_t, H)
-        gather_pieces(d_bytes[:, H:], ds_runs, k2_t, H)
+
+        sums = []
+
+        def sum_and_difference(u, freed):
+            both = sbuf("sums%d" % u, 2 * S, F32, tag=freed)
+            picked = pairs[u][:].rearrange("p (t e w) -> p e t w", e=2, w=W)
+            made = both[:].rearrange("p (t e w) -> p e t w", e=2, w=W)
+            nc.vector.tensor_tensor(made[:, 0], picked[:, 0], picked[:, 1], ALU.add)
+            nc.vector.tensor_tensor(made[:, 1], picked[:, 0], picked[:, 1], ALU.subtract)
+            sums.extend([both[:, :S], both[:, S:]])
+
+        sum_and_difference(0, "xw")
+        d_bytes = sbuf("d_bytes", 2 * H, U8, tag="pairs0")
+        nc.vector.tensor_copy(d_bytes[:, :H], ds_runs[:].indirect(k1_t[:]))
+        nc.vector.tensor_copy(d_bytes[:, H:], ds_runs[:].indirect(k2_t[:]))
+        sum_and_difference(1, "ds_runs")
+
+        def put_sums(t):
+            nc.scalar.activation(dt[t][:].indirect(n1_t[:]), sums[t][:, :W], ACT.Copy)
+
+        def put_differences(t):
+            nc.scalar.activation(dt[t][:].indirect(n2_t[:]), sums[t][:, W:], ACT.Copy)
+
+        def fetch_partner(t, lo, hi):
+            nc.scalar.activation(h_win[t][:, S + lo : S + hi], dt[t][:].indirect(n3_t[:, lo // 16 : hi // 16]), ACT.Copy)
+
+        for t in range(2):
+            put_sums(t)
+        for t in range(2):
+            put_differences(t)
+        for t in range(2, PACK):
+            put_sums(t)
+            fetch_partner(t - 2, 0, S)
+            put_differences(t)
+        fetch_partner(last - 1, 0, S)
+        fetch_partner(last, 0, HALF)
+        fetch_partner(last, HALF, S)
+
+        place_run_rows(hz_plane, hz_bytes)
         d_bytes_dealt = sbuf("d_bytes_dealt", 2 * H, U8)
-        for a in range(2):
-            nc.vector.tensor_copy(
-                d_bytes_dealt[:, a * H : (a + 1) * H].rearrange("p (t c i) -> p c t i", t=PACK, i=16),
-                d_bytes[:, a * H : (a + 1) * H].rearrange("p (c i t) -> p c t i", t=PACK, i=16),
-            )
+        nc.vector.tensor_copy(
+            d_bytes_dealt[:].bitcast(I32).rearrange("p (m t c i) -> p m c t i", m=2, t=PACK, i=4),
+            d_bytes[:].bitcast(I32).rearrange("p (m c i t) -> p m c t i", m=2, t=PACK, i=4),
+        )
         place_run_rows(d_plane, d_bytes_dealt)
         d_dealt = []
-        for name, codes in (("d2", k2_t), ("d1", k1_t)):
-            picked = sbuf(name + "_picked", H, U32)
-            gather_pieces(picked, dw, codes, H)
+        for name, codes, freed in (("d2", k2_t, "pairs1"), ("d1", k1_t, "pairs0")):
+            picked = sbuf(name + "_picked", H, U32, tag=freed)
+            nc.vector.tensor_copy(picked[:], dw[:].indirect(codes[:]))
             dealt = sbuf(name + "_dealt", H, U32)
             nc.vector.tensor_copy(
-                dealt[:].bitcast(I32).rearrange("p (t c i) -> p c t i", t=PACK, i=4),
-                picked[:].bitcast(I32).rearrange("p (c i t) -> p c t i", t=PACK, i=4),
+                dealt[:].bitcast(I32).rearrange("p (t a b) -> p t a b", t=PACK, b=4),
+                picked[:].bitcast(I32).rearrange("p (a t b) -> p t a b", t=PACK, b=4),
             )
             d_dealt.append(dealt)
         d2_dealt, d1_dealt = d_dealt
+
+        sl_t = sbuf("sl_t", PACK, F32)
+        th_t = sbuf("th_t", PACK, F32)
+        with nc.allow_non_contiguous_dma(reason="one value a row"):
+            for tile, source in ((sl_t, sl), (th_t, th)):
+                by_place = source.rearrange("(a t b) o -> b a (t o)", t=PACK, b=4)
+                for b in range(4):
+                    nc.sync.dma_start(tile[b:P:4, :], by_place[b])
         slope_times_threshold = sbuf("slope_times_threshold", PACK, F32)
         bias = sbuf("bias", PACK, F32)
         nc.gpsimd.tensor_tensor(slope_times_threshold[:], sl_t[:], th_t[:], ALU.mult)
         nc.gpsimd.tensor_scalar(bias[:], slope_times_threshold[:], -1.0, 0.0, ALU.mult, ALU.add)
+
+        larger = sbuf("larger", PACK * S, F32, tag="dw")
+
+        def weigh(t, lo, hi):
+            mine = larger[:, t * S + lo : t * S + hi]
+            nc.vector.tensor_tensor(mine, dt[t][:, lo:hi], h_win[t][:, S + lo : S + hi], ALU.max)
+            nc.vector.tensor_scalar(z_planes[:, t, lo:hi], mine, gs_t[:, t : t + 1], None, ALU.mult)
+
+        for t in range(last):
+            weigh(t, 0, S)
 
         h_banks = [psum.tile([P, S], F32, name="h_bank%d" % t) for t in range(PACK)]
         for t in range(PACK):
@@ -221,29 +242,28 @@ def tile_picked_cmixhhaarhehh_none_p_kernel(
                 stop=False,
             )
 
-        for half in range(2):
-            lo, hi = half * HALF, (half + 1) * HALF
-            weigh(last, lo, hi)
-            z_grouped = sbuf("z_grouped%d" % half, HALF * PACK, BF16)
-            nc.vector.tensor_copy(
-                z_grouped[:].rearrange("p (c i t) -> p c t i", t=PACK, i=4),
-                z_planes[:, :, lo:hi].rearrange("p t (c i) -> p c t i", i=4),
+        weigh(last, 0, HALF)
+        weigh(last, HALF, S)
+        z_words = sbuf("z_words", S, U32)
+        z_scales = sbuf("z_scales", S, U8)
+        for lo, hi in ((0, HALF), (HALF, S)):
+            nc.vector.quantize_mx(
+                out=z_words[:, lo:hi].bitcast(FP8X4),
+                scales=z_scales[:, lo:hi],
+                in_=z_grouped[:, lo * PACK : hi * PACK],
             )
-            z_words = sbuf("z_words%d" % half, HALF, U32)
-            z_scales = sbuf("z_scales%d" % half, HALF, U8)
-            nc.vector.quantize_mx(out=z_words[:].bitcast(FP8X4), scales=z_scales[:], in_=z_grouped[:])
-            for t in range(PACK):
-                nc.tensor.matmul_mx(
-                    out=h_banks[t][:, lo:hi],
-                    lhsT=d1_dealt[:, t * P : (t + 1) * P].bitcast(FP8X4),
-                    lhsT_scale=d_plane[:, t * P : (t + 1) * P],
-                    rhs=z_words[:].bitcast(FP8X4),
-                    rhs_scale=z_scales[:],
-                    start=False,
-                    stop=(half == 1),
-                )
+        for t in range(PACK):
+            nc.tensor.matmul_mx(
+                out=h_banks[t][:],
+                lhsT=d1_dealt[:, t * P : (t + 1) * P].bitcast(FP8X4),
+                lhsT_scale=d_plane[:, t * P : (t + 1) * P],
+                rhs=z_words[:].bitcast(FP8X4),
+                rhs_scale=z_scales[:],
+                start=False,
+                stop=True,
+            )
 
-        out_rows = out.rearrange("(p t) s -> p t s", t=PACK)
+        out_rows = out.rearrange("(a t b) s -> t a b s", t=PACK, b=4)
         gates = [sbuf("gates%d" % t, S, F32) for t in range(PACK)]
         result = [sbuf("result%d" % t, S, F32) for t in range(PACK)]
 
@@ -255,19 +275,20 @@ def tile_picked_cmixhhaarhehh_none_p_kernel(
             nc.scalar.activation(st_win[t][:, S:], h_win[t][:].indirect(n4_t[:]), ACT.Copy)
             nc.vector.tensor_tensor(st_win[t][:, :S], h_win[t][:, :S], st_win[t][:, S:], ALU.max)
 
-        def gate_and_store(t):
+        def gate_and_store(t, lo, hi):
             nc.scalar.activation(
-                gates[t][:],
-                st_win[t][:].indirect(n5_t[:]),
+                gates[t][:, lo:hi],
+                st_win[t][:].indirect(n5_t[:, lo // 16 : hi // 16]),
                 ACT.Sigmoid,
                 bias=bias[:, t : t + 1],
                 scale=sl_t[:, t : t + 1],
             )
-            nc.vector.tensor_tensor(result[t][:], st_win[t][:, :S], gates[t][:], ALU.mult)
-            nc.sync.dma_start(out_rows[:, t, :], result[t][:])
+            nc.vector.tensor_tensor(result[t][:, lo:hi], st_win[t][:, lo:hi], gates[t][:, lo:hi], ALU.mult)
+            nc.sync.dma_start(out_rows[t][:, :, lo:hi], result[t][:, lo:hi])
 
         take_larger(0)
-        for t in range(PACK):
-            if t < last:
-                take_larger(t + 1)
-            gate_and_store(t)
+        for t in range(last):
+            take_larger(t + 1)
+            gate_and_store(t, 0, S)
+        gate_and_store(last, 0, HALF)
+        gate_and_store(last, HALF, S)

@@ -76,14 +76,14 @@ def tile_picked_cmixhhaarhehh_none_p_kernel(
         for r in range(PACK):
             load_scale_rows(w1s, w1_scales, r)
         n1_t = load_list("n1_t", n1)
+        ds_runs = sbuf("ds_runs", G, U8)
+        load_run_rows(ds_runs, d_scales)
+        k1_t = load_list("k1_t", k1)
         n2_t = load_list("n2_t", n2)
         n3_t = load_list("n3_t", n3)
         hz_t = load_list("hz_t", hz)
         xs_runs = sbuf("xs_runs", T, U8)
         load_run_rows(xs_runs, x_scales)
-        ds_runs = sbuf("ds_runs", G, U8)
-        load_run_rows(ds_runs, d_scales)
-        k1_t = load_list("k1_t", k1)
         k2_t = load_list("k2_t", k2)
         dw = sbuf("dw", G, U32)
         nc.sync.dma_start(dw[:].bitcast(I32), d_words[0].rearrange("p n t -> p (n t)").bitcast(I32))
@@ -162,11 +162,11 @@ def tile_picked_cmixhhaarhehh_none_p_kernel(
             nc.vector.tensor_tensor(made[:, 1], picked[:, 0], picked[:, 1], ALU.subtract)
             sums.extend([both[:, :S], both[:, S:]])
 
-        sum_and_difference(0, "xw")
-        d_bytes = sbuf("d_bytes", 2 * H, U8, tag="pairs0")
+        sum_and_difference(0, None)
+        d_bytes = sbuf("d_bytes", 2 * H, U8)
         nc.vector.tensor_copy(d_bytes[:, :H], ds_runs[:].indirect(k1_t[:]))
         nc.vector.tensor_copy(d_bytes[:, H:], ds_runs[:].indirect(k2_t[:]))
-        sum_and_difference(1, "ds_runs")
+        sum_and_difference(1, None)
 
         def put_sums(t):
             nc.scalar.activation(dt[t][:].indirect(n1_t[:]), sums[t][:, :W], ACT.Copy)
@@ -181,11 +181,14 @@ def tile_picked_cmixhhaarhehh_none_p_kernel(
             put_sums(t)
         for t in range(2):
             put_differences(t)
-        for t in range(2, PACK):
-            put_sums(t)
-            fetch_partner(t - 2, 0, S)
-            put_differences(t)
-        fetch_partner(last - 1, 0, S)
+        put_sums(2)
+        fetch_partner(0, 0, S)
+        put_differences(2)
+        fetch_partner(1, 0, S)
+        put_sums(last)
+        fetch_partner(2, 0, HALF)
+        put_differences(last)
+        fetch_partner(2, HALF, S)
         fetch_partner(last, 0, HALF)
         fetch_partner(last, HALF, S)
 
@@ -197,7 +200,7 @@ def tile_picked_cmixhhaarhehh_none_p_kernel(
         )
         place_run_rows(d_plane, d_bytes_dealt)
         d_dealt = []
-        for name, codes, freed in (("d2", k2_t, "pairs1"), ("d1", k1_t, "pairs0")):
+        for name, codes, freed in (("d2", k2_t, "pairs1"), ("d1", k1_t, "d_bytes")):
             picked = sbuf(name + "_picked", H, U32, tag=freed)
             nc.vector.tensor_copy(picked[:], dw[:].indirect(codes[:]))
             dealt = sbuf(name + "_dealt", H, U32)
@@ -227,20 +230,30 @@ def tile_picked_cmixhhaarhehh_none_p_kernel(
             nc.vector.tensor_tensor(mine, dt[t][:, lo:hi], h_win[t][:, S + lo : S + hi], ALU.max)
             nc.vector.tensor_scalar(z_planes[:, t, lo:hi], mine, gs_t[:, t : t + 1], None, ALU.mult)
 
-        for t in range(last):
+        for t in range(2):
             weigh(t, 0, S)
+        weigh(2, 0, HALF)
+        weigh(2, HALF, S)
 
-        h_banks = [psum.tile([P, S], F32, name="h_bank%d" % t) for t in range(PACK)]
-        for t in range(PACK):
-            nc.tensor.matmul_mx(
-                out=h_banks[t][:],
-                lhsT=d2_dealt[:, t * P : (t + 1) * P].bitcast(FP8X4),
-                lhsT_scale=d_plane[:, H + t * P : H + (t + 1) * P],
-                rhs=hz_words[:].bitcast(FP8X4),
-                rhs_scale=hz_plane[:],
-                start=True,
-                stop=False,
-            )
+        pieces = [(0, 0, HALF), (0, HALF, S)] + [(t, 0, S) for t in range(1, PACK)]
+        h_banks = []
+        for t, lo, hi in pieces:
+            tag = "y_bank0" if hi == HALF else "h_bank%d" % t
+            h_banks.append(psum.tile([P, hi - lo], F32, name="h_bank%d_%d" % (t, lo), tag=tag))
+
+        def multiply_into_h(matrix, plane_start, words, scales, first):
+            for bank, (t, lo, hi) in zip(h_banks, pieces):
+                nc.tensor.matmul_mx(
+                    out=bank[:],
+                    lhsT=matrix[:, t * P : (t + 1) * P].bitcast(FP8X4),
+                    lhsT_scale=d_plane[:, plane_start + t * P : plane_start + (t + 1) * P],
+                    rhs=words[:, lo:hi].bitcast(FP8X4),
+                    rhs_scale=scales[:, lo:hi],
+                    start=first,
+                    stop=not first,
+                )
+
+        multiply_into_h(d2_dealt, H, hz_words, hz_plane, True)
 
         weigh(last, 0, HALF)
         weigh(last, HALF, S)
@@ -252,16 +265,7 @@ def tile_picked_cmixhhaarhehh_none_p_kernel(
                 scales=z_scales[:, lo:hi],
                 in_=z_grouped[:, lo * PACK : hi * PACK],
             )
-        for t in range(PACK):
-            nc.tensor.matmul_mx(
-                out=h_banks[t][:],
-                lhsT=d1_dealt[:, t * P : (t + 1) * P].bitcast(FP8X4),
-                lhsT_scale=d_plane[:, t * P : (t + 1) * P],
-                rhs=z_words[:].bitcast(FP8X4),
-                rhs_scale=z_scales[:],
-                start=False,
-                stop=True,
-            )
+        multiply_into_h(d1_dealt, 0, z_words, z_scales, False)
 
         out_rows = out.rearrange("(a t b) s -> t a b s", t=PACK, b=4)
         gates = [sbuf("gates%d" % t, S, F32) for t in range(PACK)]
@@ -269,9 +273,10 @@ def tile_picked_cmixhhaarhehh_none_p_kernel(
 
         def take_larger(t):
             if t == 0:
-                nc.scalar.activation(h_win[t][:, :S], h_banks[t][:], ACT.Copy, scale=0.0625)
+                nc.scalar.activation(h_win[t][:, :HALF], h_banks[0][:], ACT.Copy, scale=0.0625)
+                nc.scalar.activation(h_win[t][:, HALF:S], h_banks[1][:], ACT.Copy, scale=0.0625)
             else:
-                nc.vector.tensor_scalar(h_win[t][:, :S], h_banks[t][:], 0.0625, None, ALU.mult)
+                nc.vector.tensor_scalar(h_win[t][:, :S], h_banks[t + 1][:], 0.0625, None, ALU.mult)
             nc.scalar.activation(st_win[t][:, S:], h_win[t][:].indirect(n4_t[:]), ACT.Copy)
             nc.vector.tensor_tensor(st_win[t][:, :S], h_win[t][:, :S], st_win[t][:, S:], ALU.max)
 

@@ -40,50 +40,54 @@ def tile_picked_cmixhhaarhehh_none_p_kernel(
             nc.sync.dma_start(tile[:], source)
             return tile
 
-        def zeroed_bytes(name, cols):
+        def zeroed_bytes(name, cols, engine=nc.vector):
             tile = sbuf(name, cols, U8)
-            nc.vector.memset(tile[:].bitcast(I32), 0)
+            engine.memset(tile[:].bitcast(I32), 0)
             return tile
 
         def load_scale_rows(tile, scales, q):
-            rows = scales[0, PACK * q : PACK * (q + 1), :].bitcast(I32)
             nc.sync.dma_start(
-                tile[QUADRANT * q : QUADRANT * (q + 1), :].bitcast(I32),
-                rows.unsqueeze(0).to_broadcast([QUADRANT // PACK, PACK, rows.shape[1]]),
+                tile[QUADRANT * q : QUADRANT * q + PACK, :].bitcast(I32),
+                scales[0, PACK * q : PACK * (q + 1), :].bitcast(I32),
             )
 
         def load_run_rows(tile, scales):
-            rows = scales[0].bitcast(I32)
-            nc.sync.dma_start(tile[:].bitcast(I32), rows.unsqueeze(1).to_broadcast([16, 8, rows.shape[1]]))
+            for e in range(2):
+                nc.sync.dma_start(tile[e:P:GROUP, :].bitcast(I32), scales[0, e:16:2, :].bitcast(I32))
 
         def place_run_rows(plane, gathered):
             for u in range(2):
                 for e in range(2):
                     nc.sync.dma_start(
                         plane[2 * u + e : P : QUADRANT, :].bitcast(I32),
-                        gathered[GROUP * u + 8 * e : P : QUADRANT, :].bitcast(I32),
+                        gathered[GROUP * u + e : P : QUADRANT, :].bitcast(I32),
                     )
 
-        xs_one = sbuf("xs_one", T, U8)
-        w1s = sbuf("w1s", H, U8)
+        warm_in = sbuf("warm_in", 1, F32)
+        warm_out = sbuf("warm_out", 1, F32)
+        nc.vector.memset(warm_in[:], 0.0)
+        nc.scalar.activation(warm_out[:], warm_in[:], ACT.Sigmoid)
+
+        xs_one = zeroed_bytes("xs_one", T, nc.gpsimd)
+        w1s = zeroed_bytes("w1s", H, nc.gpsimd)
         xw = sbuf("xw", T, U32)
         w1w = sbuf("w1w", H, U16)
         offs_t = load_list("offs_t", offs)
-        for r in range(PACK):
-            load_scale_rows(xs_one, x_scales, r)
-        nc.sync.dma_start(xw[:].bitcast(I32), x_words[0].rearrange("p n t -> p (n t)").bitcast(I32))
         nc.sync.dma_start(w1w[:].bitcast(I32), w1_words[0].bitcast(I32))
-        for r in range(PACK):
-            load_scale_rows(w1s, w1_scales, r)
+        for q in range(PACK):
+            load_scale_rows(xs_one, x_scales, q)
+        nc.sync.dma_start(xw[:].bitcast(I32), x_words[0].rearrange("p n t -> p (n t)").bitcast(I32))
+        for q in range(PACK):
+            load_scale_rows(w1s, w1_scales, q)
         n1_t = load_list("n1_t", n1)
-        ds_runs = sbuf("ds_runs", G, U8)
-        load_run_rows(ds_runs, d_scales)
-        k1_t = load_list("k1_t", k1)
         n2_t = load_list("n2_t", n2)
         n3_t = load_list("n3_t", n3)
         hz_t = load_list("hz_t", hz)
-        xs_runs = sbuf("xs_runs", T, U8)
+        xs_runs = zeroed_bytes("xs_runs", T)
         load_run_rows(xs_runs, x_scales)
+        ds_runs = zeroed_bytes("ds_runs", G)
+        load_run_rows(ds_runs, d_scales)
+        k1_t = load_list("k1_t", k1)
         k2_t = load_list("k2_t", k2)
         dw = sbuf("dw", G, U32)
         nc.sync.dma_start(dw[:].bitcast(I32), d_words[0].rearrange("p n t -> p (n t)").bitcast(I32))
@@ -97,11 +101,6 @@ def tile_picked_cmixhhaarhehh_none_p_kernel(
             nc.vector.memset(dt[t][:], 0.0)
         d_plane = zeroed_bytes("d_plane", 2 * H)
         hz_plane = zeroed_bytes("hz_plane", S)
-
-        warm_in = sbuf("warm_in", 1, F32)
-        warm_out = sbuf("warm_out", 1, F32)
-        nc.vector.memset(warm_in[:], 0.0)
-        nc.scalar.activation(warm_out[:], warm_in[:], ACT.Sigmoid)
 
         w1w_dealt = sbuf("w1w_dealt", H, U16)
         w1w_by_tile = w1w[:].rearrange("p (m t) -> p t m", t=PACK)
@@ -162,11 +161,11 @@ def tile_picked_cmixhhaarhehh_none_p_kernel(
             nc.vector.tensor_tensor(made[:, 1], picked[:, 0], picked[:, 1], ALU.subtract)
             sums.extend([both[:, :S], both[:, S:]])
 
-        sum_and_difference(0, None)
+        sum_and_difference(0, "xw")
         d_bytes = sbuf("d_bytes", 2 * H, U8)
         nc.vector.tensor_copy(d_bytes[:, :H], ds_runs[:].indirect(k1_t[:]))
         nc.vector.tensor_copy(d_bytes[:, H:], ds_runs[:].indirect(k2_t[:]))
-        sum_and_difference(1, None)
+        sum_and_difference(1, "xs_runs")
 
         def put_sums(t):
             nc.scalar.activation(dt[t][:].indirect(n1_t[:]), sums[t][:, :W], ACT.Copy)

from contextlib import ExitStack

import concourse.mybir as mybir

K, T, S, H, W, G = 512, 1024, 256, 512, 128, 2048
FLOPS = 2 * K * H * S * 3

F32 = mybir.dt.float32
BF16 = mybir.dt.bfloat16
I32 = mybir.dt.int32
U32 = mybir.dt.uint32
U16 = mybir.dt.uint16
U8 = mybir.dt.uint8
FP8X4 = mybir.dt.float8_e4m3fn_x4
FP4X4 = mybir.dt.float4_e2m1fn_x4
ALU = mybir.AluOpType
ACT = mybir.ActivationFunctionType

P = 128
PACK = 4
QUADRANT = 32
GROUP = 16
DT_COLS = S + 16
HALF = S // 2


def tile_picked_cmixhhaarhehh_none_p_kernel(
    tc, x_words, x_scales, w1_words, w1_scales, gs, d_words, d_scales, sl, th, offs, n1, n2, n3, k1, k2, hz, n4, n5, out
):
    nc = tc.nc
    with ExitStack() as ctx:
        keep = ctx.enter_context(tc.tile_pool(name="keep", bufs=1))
        psum = ctx.enter_context(tc.psum_pool(name="psum", bufs=1))

        def sbuf(name, cols, dtype, tag=None):
            return keep.tile([P, cols], dtype, name=name, tag=tag or name, align_bytes=64)

        def load_list(name, source):
            tile = keep.tile(list(source.shape), U16, name=name)
            nc.sync.dma_start(tile[:], source)
            return tile

        def zeroed_bytes(name, cols, engine=nc.vector):
            tile = sbuf(name, cols, U8)
            engine.memset(tile[:].bitcast(I32), 0)
            return tile

        def load_scale_rows(tile, scales, q):
            nc.sync.dma_start(
                tile[QUADRANT * q : QUADRANT * q + PACK, :].bitcast(I32),
                scales[0, PACK * q : PACK * (q + 1), :].bitcast(I32),
            )

        def load_run_rows(tile, scales):
            for e in range(2):
                nc.sync.dma_start(tile[e:P:GROUP, :].bitcast(I32), scales[0, e:16:2, :].bitcast(I32))

        def place_run_rows(plane, gathered):
            for u in range(2):
                for e in range(2):
                    nc.sync.dma_start(
                        plane[2 * u + e : P : QUADRANT, :].bitcast(I32),
                        gathered[GROUP * u + e : P : QUADRANT, :].bitcast(I32),
                    )

        warm_in = sbuf("warm_in", 1, F32)
        warm_out = sbuf("warm_out", 1, F32)
        nc.vector.memset(warm_in[:], 0.0)
        nc.scalar.activation(warm_out[:], warm_in[:], ACT.Sigmoid)

        xs_one = zeroed_bytes("xs_one", T, nc.gpsimd)
        w1s = zeroed_bytes("w1s", H, nc.gpsimd)
        xw = sbuf("xw", T, U32)
        w1w = sbuf("w1w", H, U16)
        offs_t = load_list("offs_t", offs)
        nc.sync.dma_start(w1w[:].bitcast(I32), w1_words[0].bitcast(I32))
        for q in range(PACK):
            load_scale_rows(xs_one, x_scales, q)
        nc.sync.dma_start(xw[:].bitcast(I32), x_words[0].rearrange("p n t -> p (n t)").bitcast(I32))
        for q in range(PACK):
            load_scale_rows(w1s, w1_scales, q)
        n1_t = load_list("n1_t", n1)
        n2_t = load_list("n2_t", n2)
        n3_t = load_list("n3_t", n3)
        hz_t = load_list("hz_t", hz)
        xs_runs = zeroed_bytes("xs_runs", T)
        load_run_rows(xs_runs, x_scales)
        ds_runs = zeroed_bytes("ds_runs", G)
        load_run_rows(ds_runs, d_scales)
        k1_t = load_list("k1_t", k1)
        k2_t = load_list("k2_t", k2)
        dw = sbuf("dw", G, U32)
        nc.sync.dma_start(dw[:].bitcast(I32), d_words[0].rearrange("p n t -> p (n t)").bitcast(I32))
        n4_t = load_list("n4_t", n4)
        n5_t = load_list("n5_t", n5)
        gs_t = sbuf("gs_t", PACK, F32)
        nc.gpsimd.dma_start(gs_t[:], gs.rearrange("(p t) o -> p (t o)", t=PACK))

        dt = [sbuf("dt%d" % t, DT_COLS, F32) for t in range(PACK)]
        for t in range(PACK):
            nc.vector.memset(dt[t][:], 0.0)
        d_plane = zeroed_bytes("d_plane", 2 * H)
        hz_plane = zeroed_bytes("hz_plane", S)

        w1w_dealt = sbuf("w1w_dealt", H, U16)
        w1w_by_tile = w1w[:].rearrange("p (m t) -> p t m", t=PACK)
        nc.scalar.copy(w1w_dealt[:, :P], w1w_by_tile[:, 0, :])
        nc.scalar.copy(w1w_dealt[:, P:].rearrange("p (t m) -> p t m", m=P), w1w_by_tile[:, 1:, :])
        w1s_dealt = sbuf("w1s_dealt", H, U8)
        w1s_by_tile = w1s[:].rearrange("p (m t) -> p t m", t=PACK)
        nc.vector.tensor_copy(w1s_dealt[:, :P], w1s_by_tile[:, 0, :])
        nc.vector.tensor_copy(w1s_dealt[:, P:].rearrange("p (t m) -> p t m", m=P), w1s_by_tile[:, 1:, :])
        xq_scales = sbuf("xq_scales", S, U8)
        xq_words = sbuf("xq_words", S, U32)
        nc.vector.tensor_copy(xq_scales[:], xs_one[:].indirect(offs_t[:]))
        nc.vector.tensor_copy(xq_words[:], xw[:].indirect(offs_t[:]))

        y = [sbuf("y%d" % t, S, F32) for t in range(PACK)]
        h_win = [sbuf("h_win%d" % t, 2 * S, F32) for t in range(PACK)]
        st_win = [sbuf("st_win%d" % t, 2 * S, F32) for t in range(PACK)]
        pairs = [sbuf("pairs%d" % u, 2 * S, F32) for u in range(2)]
        z_grouped = sbuf("z_grouped", S * PACK, BF16)
        z_planes = z_grouped[:].rearrange("p (s t) -> p t s", t=PACK)

        def project(t):
            bank = psum.tile([P, S], F32, name="y_bank%d" % t)
            nc.tensor.matmul_mx(
                out=bank[:],
                lhsT=w1w_dealt[:, t * P : (t + 1) * P].bitcast(FP4X4),
                lhsT_scale=w1s_dealt[:, t * P : (t + 1) * P],
                rhs=xq_words[:].bitcast(FP8X4),
                rhs_scale=xq_scales[:],
                start=True,
                stop=True,
            )
            if t == 0:
                nc.scalar.copy(y[t][:], bank[:])
            else:
                nc.vector.tensor_copy(y[t][:], bank[:])

        for t in range(PACK):
            project(t)
        last = PACK - 1
        for t in range(PACK):
            u, start = t // 2, t % 2 * S
            nc.scalar.activation(pairs[u][:, start : start + W], y[t][:].indirect(n1_t[:]), ACT.Copy)
            nc.scalar.activation(pairs[u][:, start + W : start + S], y[t][:].indirect(n2_t[:]), ACT.Copy)

        hz_bytes = sbuf("hz_bytes", S, U8)
        nc.vector.tensor_copy(hz_bytes[:], xs_runs[:].indirect(hz_t[:]))
        hz_words = sbuf("hz_words", S, U32)
        nc.vector.tensor_copy(hz_words[:], xw[:].indirect(hz_t[:]))

        sums = []

        def sum_and_difference(u, freed):
            both = sbuf("sums%d" % u, 2 * S, F32, tag=freed)
            picked = pairs[u][:].rearrange("p (t e w) -> p e t w", e=2, w=W)
            made = both[:].rearrange("p (t e w) -> p e t w", e=2, w=W)
            nc.vector.tensor_tensor(made[:, 0], picked[:, 0], picked[:, 1], ALU.add)
            nc.vector.tensor_tensor(made[:, 1], picked[:, 0], picked[:, 1], ALU.subtract)
            sums.extend([both[:, :S], both[:, S:]])

        sum_and_difference(0, "xw")
        d_bytes = sbuf("d_bytes", 2 * H, U8)
        nc.vector.tensor_copy(d_bytes[:, :H], ds_runs[:].indirect(k1_t[:]))
        nc.vector.tensor_copy(d_bytes[:, H:], ds_runs[:].indirect(k2_t[:]))
        sum_and_difference(1, "xs_runs")

        def put_sums(t):
            nc.scalar.activation(dt[t][:].indirect(n1_t[:]), sums[t][:, :W], ACT.Copy)

        def put_differences(t):
            nc.scalar.activation(dt[t][:].indirect(n2_t[:]), sums[t][:, W:], ACT.Copy)

        def fetch_partner(t, lo, hi):
            nc.scalar.activation(h_win[t][:, S + lo : S + hi], dt[t][:].indirect(n3_t[:, lo // 16 : hi // 16]), ACT.Copy)

        for t in range(2):
            put_sums(t)
        for t in range(2):
            put_differences(t)
        put_sums(2)
        fetch_partner(0, 0, S)
        put_differences(2)
        fetch_partner(1, 0, S)
        put_sums(last)
        fetch_partner(2, 0, HALF)
        put_differences(last)
        fetch_partner(2, HALF, S)
        fetch_partner(last, 0, HALF)
        fetch_partner(last, HALF, S)

        place_run_rows(hz_plane, hz_bytes)
        d_bytes_dealt = sbuf("d_bytes_dealt", 2 * H, U8)
        nc.vector.tensor_copy(
            d_bytes_dealt[:].bitcast(I32).rearrange("p (m t c i) -> p m c t i", m=2, t=PACK, i=4),
            d_bytes[:].bitcast(I32).rearrange("p (m c i t) -> p m c t i", m=2, t=PACK, i=4),
        )
        place_run_rows(d_plane, d_bytes_dealt)
        d_dealt = []
        for name, codes, freed in (("d2", k2_t, "pairs1"), ("d1", k1_t, "d_bytes")):
            picked = sbuf(name + "_picked", H, U32, tag=freed)
            nc.vector.tensor_copy(picked[:], dw[:].indirect(codes[:]))
            dealt = sbuf(name + "_dealt", H, U32)
            nc.vector.tensor_copy(
                dealt[:].bitcast(I32).rearrange("p (t a b) -> p t a b", t=PACK, b=4),
                picked[:].bitcast(I32).rearrange("p (a t b) -> p t a b", t=PACK, b=4),
            )
            d_dealt.append(dealt)
        d2_dealt, d1_dealt = d_dealt

        sl_t = sbuf("sl_t", PACK, F32)
        th_t = sbuf("th_t", PACK, F32)
        with nc.allow_non_contiguous_dma(reason="one value a row"):
            for tile, source in ((sl_t, sl), (th_t, th)):
                by_place = source.rearrange("(a t b) o -> b a (t o)", t=PACK, b=4)
                for b in range(4):
                    nc.sync.dma_start(tile[b:P:4, :], by_place[b])
        slope_times_threshold = sbuf("slope_times_threshold", PACK, F32)
        bias = sbuf("bias", PACK, F32)
        nc.gpsimd.tensor_tensor(slope_times_threshold[:], sl_t[:], th_t[:], ALU.mult)
        nc.gpsimd.tensor_scalar(bias[:], slope_times_threshold[:], -1.0, 0.0, ALU.mult, ALU.add)

        larger = sbuf("larger", PACK * S, F32, tag="dw")

        def weigh(t, lo, hi):
            mine = larger[:, t * S + lo : t * S + hi]
            nc.vector.tensor_tensor(mine, dt[t][:, lo:hi], h_win[t][:, S + lo : S + hi], ALU.max)
            nc.vector.tensor_scalar(z_planes[:, t, lo:hi], mine, gs_t[:, t : t + 1], None, ALU.mult)

        for t in range(2):
            weigh(t, 0, S)
        weigh(2, 0, HALF)
        weigh(2, HALF, S)

        pieces = [(0, 0, HALF), (0, HALF, S)] + [(t, 0, S) for t in range(1, PACK)]
        h_banks = []
        for t, lo, hi in pieces:
            tag = "y_bank0" if hi == HALF else "h_bank%d" % t
            h_banks.append(psum.tile([P, hi - lo], F32, name="h_bank%d_%d" % (t, lo), tag=tag))

        def multiply_into_h(matrix, plane_start, words, scales, first):
            for bank, (t, lo, hi) in zip(h_banks, pieces):
                nc.tensor.matmul_mx(
                    out=bank[:],
                    lhsT=matrix[:, t * P : (t + 1) * P].bitcast(FP8X4),
                    lhsT_scale=d_plane[:, plane_start + t * P : plane_start + (t + 1) * P],
                    rhs=words[:, lo:hi].bitcast(FP8X4),
                    rhs_scale=scales[:, lo:hi],
                    start=first,
                    stop=not first,
                )

        multiply_into_h(d2_dealt, H, hz_words, hz_plane, True)

        weigh(last, 0, HALF)
        weigh(last, HALF, S)
        z_words = sbuf("z_words", S, U32)
        z_scales = sbuf("z_scales", S, U8)
        for lo, hi in ((0, HALF), (HALF, S)):
            nc.vector.quantize_mx(
                out=z_words[:, lo:hi].bitcast(FP8X4),
                scales=z_scales[:, lo:hi],
                in_=z_grouped[:, lo * PACK : hi * PACK],
            )
        multiply_into_h(d1_dealt, 0, z_words, z_scales, False)

        out_rows = out.rearrange("(a t b) s -> t a b s", t=PACK, b=4)
        gates = [sbuf("gates%d" % t, S, F32) for t in range(PACK)]
        result = [sbuf("result%d" % t, S, F32) for t in range(PACK)]

        def take_larger(t):
            if t == 0:
                nc.scalar.activation(h_win[t][:, :HALF], h_banks[0][:], ACT.Copy, scale=0.0625)
                nc.scalar.activation(h_win[t][:, HALF:S], h_banks[1][:], ACT.Copy, scale=0.0625)
            else:
                nc.vector.tensor_scalar(h_win[t][:, :S], h_banks[t + 1][:], 0.0625, None, ALU.mult)
            nc.scalar.activation(st_win[t][:, S:], h_win[t][:].indirect(n4_t[:]), ACT.Copy)
            nc.vector.tensor_tensor(st_win[t][:, :S], h_win[t][:, :S], st_win[t][:, S:], ALU.max)

        def gate_and_store(t, lo, hi):
            nc.scalar.activation(
                gates[t][:, lo:hi],
                st_win[t][:].indirect(n5_t[:, lo // 16 : hi // 16]),
                ACT.Sigmoid,
                bias=bias[:, t : t + 1],
                scale=sl_t[:, t : t + 1],
            )
            nc.vector.tensor_tensor(result[t][:, lo:hi], st_win[t][:, lo:hi], gates[t][:, lo:hi], ALU.mult)
            nc.sync.dma_start(out_rows[t][:, :, lo:hi], result[t][:, lo:hi])

        take_larger(0)
        for t in range(last):
            take_larger(t + 1)
            gate_and_store(t, 0, S)
        gate_and_store(last, 0, HALF)
        gate_and_store(last, HALF, S)
